import numpy as np
import ml_dtypes


def mxq(x, axis, fmt="e4m3"):
    dtype, down = {"e4m3": (ml_dtypes.float8_e4m3fn, 7), "e5m2": (ml_dtypes.float8_e5m2, 14)}[fmt]
    v = np.moveaxis(np.asarray(x, np.float32).astype(ml_dtypes.bfloat16).astype(np.float64), axis, -1)
    blocks = v.reshape(v.shape[:-1] + (-1, 32))
    amax = np.abs(blocks).max(-1, keepdims=True)
    byte = np.maximum(np.where(amax > 0, np.frexp(amax)[1] - 1 + 127, 0) - down, 1)
    scale = np.exp2(byte - 127.0)
    codes = (blocks / scale).astype(np.float32).astype(dtype).astype(np.float64)
    return np.moveaxis((codes * scale).reshape(v.shape), -1, axis)


WIDE = False


def mx_kscale(k):
    if not WIDE:
        return np.ones(k)
    levels = np.array([10, -10, 5, -5, 0])
    if k % 512:
        return np.exp2(np.random.permutation(np.resize(levels, k // 32))).repeat(32)
    a = np.empty((k // 512, 16))
    for p in range(k // 512):
        a[p, :8] = np.random.permutation(np.resize(levels, 8))
        for g in range(8):
            far = levels[np.abs(levels - a[p, g]) >= 10]
            a[p, g + 8] = far[np.random.randint(len(far))]
    return np.exp2(a.ravel()).repeat(32)


def f64(x):
    return np.asarray(x).astype(np.float64)


def striped(idx):
    return np.tile(idx.reshape(-1, 16).T, (8, 1)).astype(np.uint16)


def unstriped(offs):
    return offs[:16].T.reshape(-1).astype(np.int64)


E2M1 = np.array([0.0, 0.5, 1.0, 1.5, 2.0, 3.0, 4.0, 6.0, -0.0, -0.5, -1.0, -1.5, -2.0, -3.0, -4.0, -6.0])


def pack_weight(w, fmt):
    k, n = w.shape
    w = f64(np.asarray(w, np.float32).astype(ml_dtypes.bfloat16)).reshape(k // 32, 32, n)
    amax = np.abs(w).max(1)
    if fmt == "e4m3":
        byte = np.frexp(amax)[1] - 1 + 127 - 7
    else:
        mant, ex = np.frexp(amax / 6.0)
        byte = np.where(mant > 0.5, ex, ex - 1) + 127
    byte = np.clip(np.where(amax > 0, byte, 1), 1, 254)
    scaled = (w * np.exp2(127.0 - byte)[:, None, :]).reshape(k, n).astype(np.float32)
    by_word = np.ascontiguousarray(scaled.reshape(k // 512, 128, 4, n).transpose(0, 1, 3, 2))
    if fmt == "e4m3":
        words = by_word.astype(ml_dtypes.float8_e4m3fn).view(np.uint8)
    else:
        c = by_word.astype(ml_dtypes.float4_e2m1fn).view(np.uint8) & 0xF
        words = (c[..., 0::2] | (c[..., 1::2] << 4)).reshape(k // 512, 128, 2 * n)
    return np.ascontiguousarray(words), np.ascontiguousarray(byte.astype(np.uint8).reshape(k // 512, 16, n))


def unpack_weight(words, scales, fmt):
    g, _, n = scales.shape
    words = np.ascontiguousarray(words).reshape(g, 128, n, -1)
    if fmt == "e4m3":
        vals = words.view(ml_dtypes.float8_e4m3fn).astype(np.float64)
    else:
        nib = np.empty((g, 128, n, 4), np.uint8)
        nib[..., 0::2] = words & 0xF
        nib[..., 1::2] = words >> 4
        vals = E2M1[nib]
    vals = vals * np.repeat(np.exp2(scales.astype(np.float64) - 127.0), 8, axis=1)[..., None]
    return vals.transpose(0, 1, 3, 2).reshape(g * 512, n)


def gelu(v):
    return 0.5 * v * (1.0 + np.tanh(np.sqrt(2.0 / np.pi) * (v + 0.044715 * v**3)))


def bf(x):
    return np.asarray(x, np.float32).astype(ml_dtypes.bfloat16)

def planes(Y):
    n, m = Y.shape
    b = f64(bf(Y)).reshape(n // 32, 32, m)
    amax = np.abs(b).max(1)
    byte = np.clip(np.where(amax > 0, np.frexp(amax)[1] - 1 + 127 - 7, 1), 1, 254)
    codes = (b * np.exp2(127.0 - byte)[:, None, :]).reshape(n, m).astype(np.float32).astype(ml_dtypes.float8_e4m3fn).view(np.uint8)
    words = codes.reshape(n // 512, 128, 4, m).transpose(0, 1, 3, 2)
    return np.ascontiguousarray(words), np.ascontiguousarray(byte.astype(np.uint8).reshape(n // 512, 16, m))


K, KR, KW, H, T, S, T2, S2 = 2048, 1024, 1024, 512, 4096, 1024, 4096, 1536

def setup_inputs():
    n = np.random.standard_normal
    s = mx_kscale(K)[:, None]
    u = mx_kscale(H)[:, None]
    tab_words, tab_scales = pack_weight(n((K, T)) * s, "e4m3")
    tab2_words, tab2_scales = pack_weight(1.5 * n((H, T2)) / np.sqrt(H) / u, "e4m3")
    w1 = n((KR, H)) / np.sqrt(K) / s[:KR] * u.T
    w4_words, w4_scales = pack_weight(n((KW, H)) / np.sqrt(K) / s[KR:] * u.T, "e2m1")
    points = np.exp(0.8 * n(S2))
    guess = np.random.uniform(0.1, 0.35, S2)
    return {
        "tab_words": tab_words, "tab_scales": tab_scales,
        "tab2_words": tab2_words, "tab2_scales": tab2_scales,
        "offs": striped(np.random.permutation(T)[:S]),
        "offs2": striped(np.random.permutation(T2)[:S2]),
        "w1": w1.astype(np.float32),
        "w4_words": w4_words, "w4_scales": w4_scales,
        "prior": (0.5 * n(H) * u[:, 0]).astype(np.float32),
        "diff": n(S2).astype(np.float32),
        "low": (points * guess).astype(np.float32),
        "span": (points * (1.0 - guess)).astype(np.float32),
    }

def reference(tab_words, tab_scales, tab2_words, tab2_scales, offs, offs2, w1, w4_words, w4_scales, prior, diff, low, span):
    v = unpack_weight(tab_words, tab_scales, "e4m3")[:, unstriped(offs)]
    v2 = unpack_weight(tab2_words, tab2_scales, "e4m3")[:, unstriped(offs2)]
    w4 = unpack_weight(w4_words, w4_scales, "e2m1")
    h = (mxq(f64(w1), 0, "e4m3").T @ v[:KR] + w4.T @ v[KR:]) + f64(prior)[:, None]
    z = v2.T @ mxq(h, 0, "e4m3")
    p = 1.0 / (1.0 + np.exp(-(z - f64(diff)[:, None])))
    y = f64(low)[:, None] + f64(span)[:, None] * p
    words, scales = planes(y)
    return y, words, scales

@@ -1,0 +1,267 @@
+from contextlib import ExitStack
+
+import concourse.mybir as mybir
+
+F32 = mybir.dt.float32
+BF16 = mybir.dt.bfloat16
+I32 = mybir.dt.int32
+U32 = mybir.dt.uint32
+U16 = mybir.dt.uint16
+U8 = mybir.dt.uint8
+FP8X4 = mybir.dt.float8_e4m3fn_x4
+FP4X4 = mybir.dt.float4_e2m1fn_x4
+ACT = mybir.ActivationFunctionType
+ALU = mybir.AluOpType
+
+P = 128
+PACK = 4
+K_PASS = P * PACK
+K, H, T, S, S2 = 2048, 512, 4096, 1024, 1536
+PASSES = K // K_PASS
+W1_PASSES = 2
+GROUPS = S2 // K_PASS
+QUADS = 4
+QROWS = 32
+CHUNK = 256
+CHUNKS = S // CHUNK
+HALF = 512
+HALVES = S // HALF
+LIST_COL = 16
+SPAN_ROWS = 100
+VECTOR_ROWS = 2
+
+FLOPS = 2 * (K * H * S + H * S2 * S)
+
+
+def tile_list_item_response_scores_kernel(
+    tc, tab_words, tab_scales, tab2_words, tab2_scales, offs, offs2, w1, w4_words, w4_scales,
+    prior, diff, low, span, out_0, out_1, out_2,
+):
+    nc = tc.nc
+    with ExitStack() as ctx:
+        lists = ctx.enter_context(tc.tile_pool(name="lists", bufs=1))
+        keep = ctx.enter_context(tc.tile_pool(name="keep", bufs=1))
+        stage = ctx.enter_context(tc.tile_pool(name="stage", bufs=2))
+        rows32 = ctx.enter_context(tc.tile_pool(name="rows32", bufs=6))
+        probs = ctx.enter_context(tc.tile_pool(name="probs", bufs=6))
+        psum = ctx.enter_context(tc.psum_pool(name="psum", bufs=1))
+
+        def held(name, shape, dtype):
+            return keep.tile(shape, dtype, name=name, align_bytes=64)
+
+        idx = lists.tile([P, S // LIST_COL], U16, name="idx")
+        idx2 = lists.tile([P, S2 // LIST_COL], U16, name="idx2")
+        nc.sync.dma_start(idx[:], offs)
+        nc.sync.dma_start(idx2[:], offs2)
+
+        tab_s = held("tab_s", [P, T], U8)
+        tab2_s = held("tab2_s", [P, T], U8)
+        w4_s_raw = held("w4_s_raw", [P, W1_PASSES, H], U8)
+        v_s_hi = held("v_s_hi", [P, W1_PASSES, S], U8)
+        nc.vector.memset(tab_s[:].bitcast(I32), 0)
+        nc.vector.memset(tab2_s[:].bitcast(I32), 0)
+        nc.vector.memset(w4_s_raw[:].bitcast(I32), 0)
+        nc.vector.memset(v_s_hi[:].bitcast(I32), 0)
+
+        prior_t = held("prior_t", [P, PACK], F32)
+        diff_t = held("diff_t", [P, GROUPS, PACK], F32)
+        low_t = held("low_t", [P, GROUPS, PACK], F32)
+        span_t = held("span_t", [P, GROUPS, PACK], F32)
+
+        def load_words(name, words):
+            win = held(name, [P, T], U32)
+            nc.sync.dma_start(win[:].bitcast(I32), words.rearrange("p t i -> p (t i)").bitcast(I32))
+            return win
+
+        def load_w1(a):
+            raw = rows32.tile([P, PACK, H], F32, name="w1_raw", tag="rows32")
+            nc.sync.dma_start(raw[:], w1[a * K_PASS : (a + 1) * K_PASS, :].rearrange("(p i) r -> p i r", i=PACK))
+            return raw
+
+        w1_raw = [load_w1(0)]
+        nc.sync.dma_start(prior_t[:], prior.rearrange("(p t) -> p t", t=PACK))
+        for vec_t, vec in ((diff_t, diff), (low_t, low), (span_t, span)):
+            nc.sync.dma_start(vec_t[:], vec.rearrange("(g p t) -> p g t", p=P, t=PACK))
+        w4_raw = held("w4_raw", [P, W1_PASSES, 2 * H], U8)
+        nc.sync.dma_start(w4_raw[:].bitcast(I32), w4_words.rearrange("a p c -> p a c").bitcast(I32))
+        for q in range(QUADS):
+            nc.sync.dma_start(
+                tab_s[QROWS * q : QROWS * q + 16, :].bitcast(I32),
+                tab_scales[:, 4 * q : 4 * q + 4, :].bitcast(I32),
+            )
+        w1_raw.append(load_w1(1))
+        for q in range(QUADS):
+            nc.sync.dma_start(
+                tab2_s[QROWS * q : QROWS * q + 4, :].bitcast(I32),
+                tab2_scales[0, 4 * q : 4 * q + 4, :].bitcast(I32),
+            )
+        tab_w = [load_words("tab_w0", tab_words[0])]
+        for q in range(QUADS):
+            nc.sync.dma_start(
+                w4_s_raw[QROWS * q : QROWS * q + 4, :, :].bitcast(I32),
+                w4_scales[:, 4 * q : 4 * q + 4, :].rearrange("a r c -> r a c").bitcast(I32),
+            )
+        for a in range(1, PASSES):
+            tab_w.append(load_words("tab_w%d" % a, tab_words[a]))
+        tab2_w = load_words("tab2_w", tab2_words[0])
+
+        w1_codes = held("w1_codes", [P, W1_PASSES, H], U32)
+        w1_s = held("w1_s", [P, W1_PASSES, H], U8)
+        w1_bf = []
+        for a in range(W1_PASSES):
+            grouped = stage.tile([P, H * PACK], BF16, name="w1_grouped", tag="grouped", align_bytes=64)
+            nc.scalar.activation(
+                grouped[:].rearrange("p (t m i) -> p m t i", t=PACK, i=PACK),
+                w1_raw[a][:].rearrange("p i (m t) -> p m t i", t=PACK),
+                ACT.Copy,
+            )
+            w1_bf.append(grouped)
+
+        v_s = held("v_s", [P, S], U8)
+        nc.vector.tensor_copy(v_s[:], tab_s[:].indirect(idx[:]))
+        for a in range(W1_PASSES):
+            first = 4 * (W1_PASSES + a)
+            nc.scalar.dma_start(
+                v_s_hi[0:SPAN_ROWS, a, :].bitcast(I32), v_s[first : first + SPAN_ROWS, :].bitcast(I32)
+            )
+        for a in range(W1_PASSES):
+            nc.vector.quantize_mx(out=w1_codes[:, a, :].bitcast(FP8X4), scales=w1_s[:, a, :], in_=w1_bf[a][:])
+
+        v2_s_list = held("v2_s_list", [P, S2], U8)
+        nc.vector.tensor_copy(v2_s_list[:], tab2_s[:].indirect(idx2[:]))
+        v2_s = held("v2_s", [P, GROUPS, PACK, P], U8)
+        nc.vector.tensor_copy(v2_s[:], v2_s_list[:].rearrange("p (g m t) -> p g t m", g=GROUPS, t=PACK))
+
+        shift = held("shift", [P, GROUPS, PACK], F32)
+        gain = held("gain", [P, GROUPS, PACK], F32)
+        mid = held("mid", [P, GROUPS, PACK], F32)
+        nc.vector.tensor_scalar(shift[:], diff_t[:], -0.5, None, ALU.mult)
+        nc.vector.tensor_scalar(gain[:], span_t[:], 0.5, None, ALU.mult)
+        nc.vector.tensor_tensor(mid[:], gain[:], low_t[:], ALU.add)
+
+        w4_codes = held("w4_codes", [P, W1_PASSES, PACK, 2 * P], U8)
+        w4_s = held("w4_s", [P, W1_PASSES, PACK, P], U8)
+        nc.vector.tensor_copy(
+            w4_codes[:].bitcast(U16), w4_raw[:].bitcast(U16).rearrange("p a (m t) -> p a t m", t=PACK)
+        )
+        nc.vector.tensor_copy(w4_s[:], w4_s_raw[:].rearrange("p a (m t) -> p a t m", t=PACK))
+
+        banks = [psum.tile([P, 2, CHUNK], F32, name="bank%d" % b) for b in range(2 * CHUNKS)]
+
+        def first_product(a, c, v_w):
+            cols = slice(c * CHUNK, (c + 1) * CHUNK)
+            for t in range(PACK):
+                if a < W1_PASSES:
+                    lhsT = w1_codes[:, a, t * P : (t + 1) * P].bitcast(FP8X4)
+                    lhsT_scale = w1_s[:, a, t * P : (t + 1) * P]
+                    rhs_scale = v_s[4 * a : P, cols]
+                else:
+                    lhsT = w4_codes[:, a - W1_PASSES, t, :].bitcast(FP4X4)
+                    lhsT_scale = w4_s[:, a - W1_PASSES, t, :]
+                    rhs_scale = v_s_hi[:, a - W1_PASSES, cols]
+                nc.tensor.matmul_mx(
+                    out=banks[2 * c + t // 2][:, t % 2, :],
+                    lhsT=lhsT, lhsT_scale=lhsT_scale,
+                    rhs=v_w[:, cols].bitcast(FP8X4), rhs_scale=rhs_scale,
+                    start=(a == 0 and t % 2 == 0), stop=(a == PASSES - 1 and t % 2 == 1),
+                )
+
+        for a in range(PASSES - 1):
+            v_w = held("v_w%d" % a, [P, S], U32)
+            nc.vector.tensor_copy(v_w[:], tab_w[a][:].indirect(idx[:]))
+            for c in range(CHUNKS):
+                first_product(a, c, v_w)
+        last = PASSES - 1
+        v_w = held("v_w%d" % last, [P, S], U32)
+        h_bf = []
+        for c in range(CHUNKS):
+            lc = CHUNK // LIST_COL
+            nc.vector.tensor_copy(
+                v_w[:, c * CHUNK : (c + 1) * CHUNK], tab_w[last][:].indirect(idx[:, c * lc : (c + 1) * lc])
+            )
+            first_product(last, c, v_w)
+            rows = held("h_bf%d" % c, [P, PACK, CHUNK], BF16)
+            for t in range(PACK):
+                nc.scalar.activation(
+                    rows[:, t, :], banks[2 * c + t // 2][:, t % 2, :], ACT.Identity, bias=prior_t[:, t : t + 1]
+                )
+            h_bf.append(rows)
+
+        h_codes = held("h_codes", [P, S], U32)
+        h_s = held("h_s", [P, S], U8)
+
+        def interleave(dst, rows):
+            nc.vector.tensor_copy(
+                dst.rearrange("p (c i t) -> p c t i", i=PACK, t=PACK),
+                rows.rearrange("p t (c i) -> p c t i", i=PACK),
+            )
+
+        h_grouped = [held("h_grouped%d" % c, [P, CHUNK * PACK], BF16) for c in range(CHUNKS)]
+
+        def quantize_h(c):
+            cols = slice(c * CHUNK, (c + 1) * CHUNK)
+            nc.vector.quantize_mx(out=h_codes[:, cols].bitcast(FP8X4), scales=h_s[:, cols], in_=h_grouped[c][:])
+
+        v2_w = [held("v2_w%d" % g, [P, PACK, P], U32) for g in range(GROUPS)]
+
+        def gather_questions(g):
+            lc = K_PASS // LIST_COL
+            nc.vector.tensor_copy(
+                v2_w[g][:].rearrange("p t m -> p m t"), tab2_w[:].indirect(idx2[:, g * lc : (g + 1) * lc])
+            )
+
+        interleave(h_grouped[0][:], h_bf[0][:])
+        interleave(h_grouped[1][:], h_bf[1][:])
+        quantize_h(0)
+        quantize_h(1)
+        gather_questions(0)
+        interleave(h_grouped[2][:], h_bf[2][:])
+        interleave(h_grouped[3][:], h_bf[3][:])
+        quantize_h(2)
+        quantize_h(3)
+
+        y_s = held("y_s", [P, GROUPS, S], U8)
+        unit = 0
+        for g in range(GROUPS):
+            if g > 0:
+                gather_questions(g)
+            widths = [HALF, CHUNK, CHUNK] if g == GROUPS - 1 else [HALF, HALF]
+            first = 0
+            for width in widths:
+                cols = slice(first, first + width)
+                first += width
+                y = rows32.tile([P, PACK, width], F32, name="y", tag="rows32")
+                for t in range(PACK):
+                    z = psum.tile([P, width], F32, name="bank%d" % (PACK * (unit % 2) + t))
+                    nc.tensor.matmul_mx(
+                        out=z[:],
+                        lhsT=v2_w[g][:, t, :].bitcast(FP8X4), lhsT_scale=v2_s[:, g, t, :],
+                        rhs=h_codes[:, cols].bitcast(FP8X4), rhs_scale=h_s[:, cols],
+                        start=True, stop=True,
+                    )
+                    prob = probs.tile([P, width], F32, name="prob")
+                    nc.scalar.activation(prob[:], z[:], ACT.Tanh, bias=shift[:, g, t : t + 1], scale=0.5)
+                    if t >= VECTOR_ROWS:
+                        nc.scalar.activation(
+                            y[:, t, :], prob[:], ACT.Identity,
+                            bias=mid[:, g, t : t + 1], scale=gain[:, g, t : t + 1],
+                        )
+                    else:
+                        nc.vector.tensor_scalar(
+                            y[:, t, :], prob[:], gain[:, g, t : t + 1], mid[:, g, t : t + 1], ALU.mult, ALU.add
+                        )
+                rows = out_0[g * K_PASS : (g + 1) * K_PASS, cols].rearrange("(p t) j -> p t j", t=PACK)
+                nc.sync.dma_start(rows, y[:])
+                y_grouped = stage.tile([P, width * PACK], BF16, name="y_grouped", tag="grouped", align_bytes=64)
+                interleave(y_grouped[:], y[:])
+                y_codes = held("y_codes%d" % unit, [P, width], U32)
+                nc.vector.quantize_mx(out=y_codes[:].bitcast(FP8X4), scales=y_s[:, g, cols], in_=y_grouped[:])
+                nc.sync.dma_start(
+                    out_1[g, :, cols, :].rearrange("p j t -> p (j t)").bitcast(I32), y_codes[:].bitcast(I32)
+                )
+                unit += 1
+        for q in range(QUADS):
+            nc.scalar.dma_start(
+                out_2[:, 4 * q : 4 * q + 4, :].rearrange("g r j -> r g j").bitcast(I32),
+                y_s[QROWS * q : QROWS * q + 4, :, :].bitcast(I32),
+            )

@@ -1,6 +1,7 @@
 from contextlib import ExitStack
 
 import concourse.mybir as mybir
+from concourse.masks import make_identity
 
 F32 = mybir.dt.float32
 BF16 = mybir.dt.bfloat16
@@ -29,6 +30,8 @@ HALVES = S // HALF
 LIST_COL = 16
 SPAN_ROWS = 100
 VECTOR_ROWS = 2
+VEC_ROWS = 1 + 3 * GROUPS
+VEC_FIRST = QROWS - VEC_ROWS
 
 FLOPS = 2 * (K * H * S + H * S2 * S)
 
@@ -43,7 +46,7 @@ def tile_list_item_response_scores_kernel(
         keep = ctx.enter_context(tc.tile_pool(name="keep", bufs=1))
         stage = ctx.enter_context(tc.tile_pool(name="stage", bufs=2))
         rows32 = ctx.enter_context(tc.tile_pool(name="rows32", bufs=6))
-        probs = ctx.enter_context(tc.tile_pool(name="probs", bufs=6))
+        probs = ctx.enter_context(tc.tile_pool(name="probs", bufs=8))
         psum = ctx.enter_context(tc.psum_pool(name="psum", bufs=1))
 
         def held(name, shape, dtype):
@@ -58,18 +61,21 @@ def tile_list_item_response_scores_kernel(
         tab2_s = held("tab2_s", [P, T], U8)
         w4_s_raw = held("w4_s_raw", [P, W1_PASSES, H], U8)
         v_s_hi = held("v_s_hi", [P, W1_PASSES, S], U8)
+        v2_s = held("v2_s", [P, S2], U8)
+        vec_rows = held("vec_rows", [P, K_PASS], F32)
         nc.vector.memset(tab_s[:].bitcast(I32), 0)
-        nc.vector.memset(tab2_s[:].bitcast(I32), 0)
+        nc.gpsimd.memset(tab2_s[:].bitcast(I32), 0)
         nc.vector.memset(w4_s_raw[:].bitcast(I32), 0)
+        nc.gpsimd.memset(vec_rows[0:VEC_FIRST, :], 0.0)
+        nc.gpsimd.memset(vec_rows[QROWS : 2 * QROWS, :], 0.0)
+        nc.gpsimd.memset(vec_rows[2 * QROWS : P, :], 0.0)
         nc.vector.memset(v_s_hi[:].bitcast(I32), 0)
+        nc.vector.memset(v2_s[:].bitcast(I32), 0)
+        ident = held("ident", [P, P], F32)
+        make_identity(nc, ident[:])
 
-        prior_t = held("prior_t", [P, PACK], F32)
-        diff_t = held("diff_t", [P, GROUPS, PACK], F32)
-        low_t = held("low_t", [P, GROUPS, PACK], F32)
-        span_t = held("span_t", [P, GROUPS, PACK], F32)
-
-        def load_words(name, words):
-            win = held(name, [P, T], U32)
+        def load_words(name, words, slot):
+            win = keep.tile([P, T], U32, name=name, tag=slot, align_bytes=64)
             nc.sync.dma_start(win[:].bitcast(I32), words.rearrange("p t i -> p (t i)").bitcast(I32))
             return win
 
@@ -79,31 +85,33 @@ def tile_list_item_response_scores_kernel(
             return raw
 
         w1_raw = [load_w1(0)]
-        nc.sync.dma_start(prior_t[:], prior.rearrange("(p t) -> p t", t=PACK))
-        for vec_t, vec in ((diff_t, diff), (low_t, low), (span_t, span)):
-            nc.sync.dma_start(vec_t[:], vec.rearrange("(g p t) -> p g t", p=P, t=PACK))
+        nc.sync.dma_start(vec_rows[VEC_FIRST : VEC_FIRST + 1, :], prior.rearrange("(g c) -> g c", g=1))
+        for n, vec in enumerate((diff, low, span)):
+            row = VEC_FIRST + 1 + GROUPS * n
+            nc.sync.dma_start(vec_rows[row : row + GROUPS, :], vec.rearrange("(g c) -> g c", g=GROUPS))
         w4_raw = held("w4_raw", [P, W1_PASSES, 2 * H], U8)
         nc.sync.dma_start(w4_raw[:].bitcast(I32), w4_words.rearrange("a p c -> p a c").bitcast(I32))
+        nc.sync.dma_start(tab2_s[0:P:8, :].bitcast(I32), tab2_scales[0].bitcast(I32))
         for q in range(QUADS):
             nc.sync.dma_start(
                 tab_s[QROWS * q : QROWS * q + 16, :].bitcast(I32),
                 tab_scales[:, 4 * q : 4 * q + 4, :].bitcast(I32),
             )
-        w1_raw.append(load_w1(1))
-        for q in range(QUADS):
-            nc.sync.dma_start(
-                tab2_s[QROWS * q : QROWS * q + 4, :].bitcast(I32),
-                tab2_scales[0, 4 * q : 4 * q + 4, :].bitcast(I32),
-            )
-        tab_w = [load_words("tab_w0", tab_words[0])]
         for q in range(QUADS):
             nc.sync.dma_start(
                 w4_s_raw[QROWS * q : QROWS * q + 4, :, :].bitcast(I32),
                 w4_scales[:, 4 * q : 4 * q + 4, :].rearrange("a r c -> r a c").bitcast(I32),
             )
-        for a in range(1, PASSES):
-            tab_w.append(load_words("tab_w%d" % a, tab_words[a]))
-        tab2_w = load_words("tab2_w", tab2_words[0])
+        w1_raw.append(load_w1(1))
+        tab_w = [load_words("tab_w%d" % a, tab_words[a], "tab_w%d" % a) for a in range(W1_PASSES)]
+
+        turned = psum.tile([P, PACK, P], F32, name="bank7")
+        for t in range(PACK):
+            nc.tensor.transpose(turned[:, t, :], vec_rows[:, t : K_PASS : PACK], ident[:])
+        vecs = held("vecs", [P, VEC_ROWS, PACK], F32)
+        nc.scalar.copy(vecs[:], turned[:, :, VEC_FIRST:QROWS].rearrange("p t v -> p v t"))
+        prior_t = vecs[:, 0, :]
+        diff_t, low_t, span_t = [vecs[:, 1 + GROUPS * n : 1 + GROUPS * (n + 1), :] for n in range(3)]
 
         w1_codes = held("w1_codes", [P, W1_PASSES, H], U32)
         w1_s = held("w1_s", [P, W1_PASSES, H], U8)
@@ -121,29 +129,25 @@ def tile_list_item_response_scores_kernel(
         nc.vector.tensor_copy(v_s[:], tab_s[:].indirect(idx[:]))
         for a in range(W1_PASSES):
             first = 4 * (W1_PASSES + a)
-            nc.scalar.dma_start(
+            nc.sync.dma_start(
                 v_s_hi[0:SPAN_ROWS, a, :].bitcast(I32), v_s[first : first + SPAN_ROWS, :].bitcast(I32)
             )
+        tab_w.append(load_words("tab_w2", tab_words[2], "tab_s"))
         for a in range(W1_PASSES):
             nc.vector.quantize_mx(out=w1_codes[:, a, :].bitcast(FP8X4), scales=w1_s[:, a, :], in_=w1_bf[a][:])
 
         v2_s_list = held("v2_s_list", [P, S2], U8)
         nc.vector.tensor_copy(v2_s_list[:], tab2_s[:].indirect(idx2[:]))
-        v2_s = held("v2_s", [P, GROUPS, PACK, P], U8)
-        nc.vector.tensor_copy(v2_s[:], v2_s_list[:].rearrange("p (g m t) -> p g t m", g=GROUPS, t=PACK))
+        tab_w.append(load_words("tab_w3", tab_words[3], "tab2_s"))
 
         shift = held("shift", [P, GROUPS, PACK], F32)
         gain = held("gain", [P, GROUPS, PACK], F32)
         mid = held("mid", [P, GROUPS, PACK], F32)
-        nc.vector.tensor_scalar(shift[:], diff_t[:], -0.5, None, ALU.mult)
-        nc.vector.tensor_scalar(gain[:], span_t[:], 0.5, None, ALU.mult)
-        nc.vector.tensor_tensor(mid[:], gain[:], low_t[:], ALU.add)
+        nc.vector.tensor_scalar(shift[:], diff_t, -0.5, None, ALU.mult)
+        nc.vector.tensor_scalar(gain[:], span_t, 0.5, None, ALU.mult)
+        nc.vector.tensor_tensor(mid[:], gain[:], low_t, ALU.add)
 
-        w4_codes = held("w4_codes", [P, W1_PASSES, PACK, 2 * P], U8)
         w4_s = held("w4_s", [P, W1_PASSES, PACK, P], U8)
-        nc.vector.tensor_copy(
-            w4_codes[:].bitcast(U16), w4_raw[:].bitcast(U16).rearrange("p a (m t) -> p a t m", t=PACK)
-        )
         nc.vector.tensor_copy(w4_s[:], w4_s_raw[:].rearrange("p a (m t) -> p a t m", t=PACK))
 
         banks = [psum.tile([P, 2, CHUNK], F32, name="bank%d" % b) for b in range(2 * CHUNKS)]
@@ -166,11 +170,31 @@ def tile_list_item_response_scores_kernel(
                     start=(a == 0 and t % 2 == 0), stop=(a == PASSES - 1 and t % 2 == 1),
                 )
 
-        for a in range(PASSES - 1):
+        def whole_pass(a):
             v_w = held("v_w%d" % a, [P, S], U32)
-            nc.vector.tensor_copy(v_w[:], tab_w[a][:].indirect(idx[:]))
+            lc = HALF // LIST_COL
+            for half in range(HALVES):
+                nc.vector.tensor_copy(
+                    v_w[:, half * HALF : (half + 1) * HALF], tab_w[a][:].indirect(idx[:, half * lc : (half + 1) * lc])
+                )
             for c in range(CHUNKS):
                 first_product(a, c, v_w)
+
+        whole_pass(0)
+        v2_s_dealt = keep.tile([P, GROUPS, PACK, P], U8, name="v2_s_dealt", tag="tab_w0", align_bytes=64)
+        nc.vector.tensor_copy(v2_s_dealt[:], v2_s_list[:].rearrange("p (g m t) -> p g t m", g=GROUPS, t=PACK))
+        for r in range(4):
+            nc.sync.dma_start(
+                v2_s[r:P:QROWS, :].bitcast(I32),
+                v2_s_dealt[:].rearrange("p g t m -> p (g t m)")[8 * r : P : QROWS, :].bitcast(I32),
+            )
+        whole_pass(1)
+        tab2_w = load_words("tab2_w", tab2_words[0], "tab_w1")
+        w4_codes = held("w4_codes", [P, W1_PASSES, PACK, 2 * P], U8)
+        nc.vector.tensor_copy(
+            w4_codes[:].bitcast(U16), w4_raw[:].bitcast(U16).rearrange("p a (m t) -> p a t m", t=PACK)
+        )
+        whole_pass(2)
         last = PASSES - 1
         v_w = held("v_w%d" % last, [P, S], U32)
         h_bf = []
@@ -235,7 +259,7 @@ def tile_list_item_response_scores_kernel(
                     z = psum.tile([P, width], F32, name="bank%d" % (PACK * (unit % 2) + t))
                     nc.tensor.matmul_mx(
                         out=z[:],
-                        lhsT=v2_w[g][:, t, :].bitcast(FP8X4), lhsT_scale=v2_s[:, g, t, :],
+                        lhsT=v2_w[g][:, t, :].bitcast(FP8X4), lhsT_scale=v2_s[:, g * K_PASS + t * P : g * K_PASS + (t + 1) * P],
                         rhs=h_codes[:, cols].bitcast(FP8X4), rhs_scale=h_s[:, cols],
                         start=True, stop=True,
                     )
@@ -260,8 +284,11 @@ def tile_list_item_response_scores_kernel(
                     out_1[g, :, cols, :].rearrange("p j t -> p (j t)").bitcast(I32), y_codes[:].bitcast(I32)
                 )
                 unit += 1
-        for q in range(QUADS):
-            nc.scalar.dma_start(
-                out_2[:, 4 * q : 4 * q + 4, :].rearrange("g r j -> r g j").bitcast(I32),
-                y_s[QROWS * q : QROWS * q + 4, :, :].bitcast(I32),
-            )
+            if g > 0:
+                done = slice(0, g + 1) if g < GROUPS - 1 else slice(g, g + 1)
+                queue = nc.sync if g < GROUPS - 1 else nc.scalar
+                for r in range(4):
+                    queue.dma_start(
+                        out_2[done, r:16:4, :].rearrange("g q j -> q g j").bitcast(I32),
+                        y_s[r:P:QROWS, done, :].bitcast(I32),
+                    )

from contextlib import ExitStack

import concourse.mybir as mybir
from concourse.masks import make_identity

F32 = mybir.dt.float32
BF16 = mybir.dt.bfloat16
I32 = mybir.dt.int32
U32 = mybir.dt.uint32
U16 = mybir.dt.uint16
U8 = mybir.dt.uint8
FP8X4 = mybir.dt.float8_e4m3fn_x4
FP4X4 = mybir.dt.float4_e2m1fn_x4
ACT = mybir.ActivationFunctionType
ALU = mybir.AluOpType

P = 128
PACK = 4
K_PASS = P * PACK
K, H, T, S, S2 = 2048, 512, 4096, 1024, 1536
PASSES = K // K_PASS
W1_PASSES = 2
GROUPS = S2 // K_PASS
QUADS = 4
QROWS = 32
CHUNK = 256
CHUNKS = S // CHUNK
HALF = 512
HALVES = S // HALF
LIST_COL = 16
SPAN_ROWS = 100
VECTOR_ROWS = 2
VEC_ROWS = 1 + 3 * GROUPS
VEC_FIRST = QROWS - VEC_ROWS

FLOPS = 2 * (K * H * S + H * S2 * S)


def tile_list_item_response_scores_kernel(
    tc, tab_words, tab_scales, tab2_words, tab2_scales, offs, offs2, w1, w4_words, w4_scales,
    prior, diff, low, span, out_0, out_1, out_2,
):
    nc = tc.nc
    with ExitStack() as ctx:
        lists = ctx.enter_context(tc.tile_pool(name="lists", bufs=1))
        keep = ctx.enter_context(tc.tile_pool(name="keep", bufs=1))
        stage = ctx.enter_context(tc.tile_pool(name="stage", bufs=2))
        rows32 = ctx.enter_context(tc.tile_pool(name="rows32", bufs=6))
        probs = ctx.enter_context(tc.tile_pool(name="probs", bufs=8))
        psum = ctx.enter_context(tc.psum_pool(name="psum", bufs=1))

        def held(name, shape, dtype):
            return keep.tile(shape, dtype, name=name, align_bytes=64)

        idx = lists.tile([P, S // LIST_COL], U16, name="idx")
        idx2 = lists.tile([P, S2 // LIST_COL], U16, name="idx2")
        nc.sync.dma_start(idx[:], offs)
        nc.sync.dma_start(idx2[:], offs2)

        tab_s = held("tab_s", [P, T], U8)
        tab2_s = held("tab2_s", [P, T], U8)
        w4_s_raw = held("w4_s_raw", [P, W1_PASSES, H], U8)
        v_s_hi = held("v_s_hi", [P, W1_PASSES, S], U8)
        v2_s = held("v2_s", [P, S2], U8)
        vec_rows = held("vec_rows", [P, K_PASS], F32)
        nc.vector.memset(tab_s[:].bitcast(I32), 0)
        nc.gpsimd.memset(tab2_s[:].bitcast(I32), 0)
        nc.vector.memset(w4_s_raw[:].bitcast(I32), 0)
        nc.gpsimd.memset(vec_rows[0:VEC_FIRST, :], 0.0)
        nc.gpsimd.memset(vec_rows[QROWS : 2 * QROWS, :], 0.0)
        nc.gpsimd.memset(vec_rows[2 * QROWS : P, :], 0.0)
        nc.vector.memset(v_s_hi[:].bitcast(I32), 0)
        nc.vector.memset(v2_s[:].bitcast(I32), 0)
        ident = held("ident", [P, P], F32)
        make_identity(nc, ident[:])

        def load_words(name, words, slot):
            win = keep.tile([P, T], U32, name=name, tag=slot, align_bytes=64)
            nc.sync.dma_start(win[:].bitcast(I32), words.rearrange("p t i -> p (t i)").bitcast(I32))
            return win

        def load_w1(a):
            raw = rows32.tile([P, PACK, H], F32, name="w1_raw", tag="rows32")
            nc.sync.dma_start(raw[:], w1[a * K_PASS : (a + 1) * K_PASS, :].rearrange("(p i) r -> p i r", i=PACK))
            return raw

        w1_raw = [load_w1(0)]
        nc.sync.dma_start(vec_rows[VEC_FIRST : VEC_FIRST + 1, :], prior.rearrange("(g c) -> g c", g=1))
        for n, vec in enumerate((diff, low, span)):
            row = VEC_FIRST + 1 + GROUPS * n
            nc.sync.dma_start(vec_rows[row : row + GROUPS, :], vec.rearrange("(g c) -> g c", g=GROUPS))
        w4_raw = held("w4_raw", [P, W1_PASSES, 2 * H], U8)
        nc.sync.dma_start(w4_raw[:].bitcast(I32), w4_words.rearrange("a p c -> p a c").bitcast(I32))
        nc.sync.dma_start(tab2_s[0:P:8, :].bitcast(I32), tab2_scales[0].bitcast(I32))
        for q in range(QUADS):
            nc.sync.dma_start(
                tab_s[QROWS * q : QROWS * q + 16, :].bitcast(I32),
                tab_scales[:, 4 * q : 4 * q + 4, :].bitcast(I32),
            )
        for q in range(QUADS):
            nc.sync.dma_start(
                w4_s_raw[QROWS * q : QROWS * q + 4, :, :].bitcast(I32),
                w4_scales[:, 4 * q : 4 * q + 4, :].rearrange("a r c -> r a c").bitcast(I32),
            )
        w1_raw.append(load_w1(1))
        tab_w = [load_words("tab_w%d" % a, tab_words[a], "tab_w%d" % a) for a in range(W1_PASSES)]

        turned = psum.tile([P, PACK, P], F32, name="bank7")
        for t in range(PACK):
            nc.tensor.transpose(turned[:, t, :], vec_rows[:, t : K_PASS : PACK], ident[:])
        vecs = held("vecs", [P, VEC_ROWS, PACK], F32)
        nc.scalar.copy(vecs[:], turned[:, :, VEC_FIRST:QROWS].rearrange("p t v -> p v t"))
        prior_t = vecs[:, 0, :]
        diff_t, low_t, span_t = [vecs[:, 1 + GROUPS * n : 1 + GROUPS * (n + 1), :] for n in range(3)]

        w1_codes = held("w1_codes", [P, W1_PASSES, H], U32)
        w1_s = held("w1_s", [P, W1_PASSES, H], U8)
        w1_bf = []
        for a in range(W1_PASSES):
            grouped = stage.tile([P, H * PACK], BF16, name="w1_grouped", tag="grouped", align_bytes=64)
            nc.scalar.activation(
                grouped[:].rearrange("p (t m i) -> p m t i", t=PACK, i=PACK),
                w1_raw[a][:].rearrange("p i (m t) -> p m t i", t=PACK),
                ACT.Copy,
            )
            w1_bf.append(grouped)

        v_s = held("v_s", [P, S], U8)
        nc.vector.tensor_copy(v_s[:], tab_s[:].indirect(idx[:]))
        for a in range(W1_PASSES):
            first = 4 * (W1_PASSES + a)
            nc.sync.dma_start(
                v_s_hi[0:SPAN_ROWS, a, :].bitcast(I32), v_s[first : first + SPAN_ROWS, :].bitcast(I32)
            )
        tab_w.append(load_words("tab_w2", tab_words[2], "tab_s"))
        for a in range(W1_PASSES):
            nc.vector.quantize_mx(out=w1_codes[:, a, :].bitcast(FP8X4), scales=w1_s[:, a, :], in_=w1_bf[a][:])

        v2_s_list = held("v2_s_list", [P, S2], U8)
        nc.vector.tensor_copy(v2_s_list[:], tab2_s[:].indirect(idx2[:]))
        tab_w.append(load_words("tab_w3", tab_words[3], "tab2_s"))

        shift = held("shift", [P, GROUPS, PACK], F32)
        gain = held("gain", [P, GROUPS, PACK], F32)
        mid = held("mid", [P, GROUPS, PACK], F32)
        nc.vector.tensor_scalar(shift[:], diff_t, -0.5, None, ALU.mult)
        nc.vector.tensor_scalar(gain[:], span_t, 0.5, None, ALU.mult)
        nc.vector.tensor_tensor(mid[:], gain[:], low_t, ALU.add)

        w4_s = held("w4_s", [P, W1_PASSES, PACK, P], U8)
        nc.vector.tensor_copy(w4_s[:], w4_s_raw[:].rearrange("p a (m t) -> p a t m", t=PACK))

        banks = [psum.tile([P, 2, CHUNK], F32, name="bank%d" % b) for b in range(2 * CHUNKS)]

        def first_product(a, c, v_w):
            cols = slice(c * CHUNK, (c + 1) * CHUNK)
            for t in range(PACK):
                if a < W1_PASSES:
                    lhsT = w1_codes[:, a, t * P : (t + 1) * P].bitcast(FP8X4)
                    lhsT_scale = w1_s[:, a, t * P : (t + 1) * P]
                    rhs_scale = v_s[4 * a : P, cols]
                else:
                    lhsT = w4_codes[:, a - W1_PASSES, t, :].bitcast(FP4X4)
                    lhsT_scale = w4_s[:, a - W1_PASSES, t, :]
                    rhs_scale = v_s_hi[:, a - W1_PASSES, cols]
                nc.tensor.matmul_mx(
                    out=banks[2 * c + t // 2][:, t % 2, :],
                    lhsT=lhsT, lhsT_scale=lhsT_scale,
                    rhs=v_w[:, cols].bitcast(FP8X4), rhs_scale=rhs_scale,
                    start=(a == 0 and t % 2 == 0), stop=(a == PASSES - 1 and t % 2 == 1),
                )

        def whole_pass(a):
            v_w = held("v_w%d" % a, [P, S], U32)
            lc = HALF // LIST_COL
            for half in range(HALVES):
                nc.vector.tensor_copy(
                    v_w[:, half * HALF : (half + 1) * HALF], tab_w[a][:].indirect(idx[:, half * lc : (half + 1) * lc])
                )
            for c in range(CHUNKS):
                first_product(a, c, v_w)

        whole_pass(0)
        v2_s_dealt = keep.tile([P, GROUPS, PACK, P], U8, name="v2_s_dealt", tag="tab_w0", align_bytes=64)
        nc.vector.tensor_copy(v2_s_dealt[:], v2_s_list[:].rearrange("p (g m t) -> p g t m", g=GROUPS, t=PACK))
        for r in range(4):
            nc.sync.dma_start(
                v2_s[r:P:QROWS, :].bitcast(I32),
                v2_s_dealt[:].rearrange("p g t m -> p (g t m)")[8 * r : P : QROWS, :].bitcast(I32),
            )
        whole_pass(1)
        tab2_w = load_words("tab2_w", tab2_words[0], "tab_w1")
        w4_codes = held("w4_codes", [P, W1_PASSES, PACK, 2 * P], U8)
        nc.vector.tensor_copy(
            w4_codes[:].bitcast(U16), w4_raw[:].bitcast(U16).rearrange("p a (m t) -> p a t m", t=PACK)
        )
        whole_pass(2)
        last = PASSES - 1
        v_w = held("v_w%d" % last, [P, S], U32)
        h_bf = []
        for c in range(CHUNKS):
            lc = CHUNK // LIST_COL
            nc.vector.tensor_copy(
                v_w[:, c * CHUNK : (c + 1) * CHUNK], tab_w[last][:].indirect(idx[:, c * lc : (c + 1) * lc])
            )
            first_product(last, c, v_w)
            rows = held("h_bf%d" % c, [P, PACK, CHUNK], BF16)
            for t in range(PACK):
                nc.scalar.activation(
                    rows[:, t, :], banks[2 * c + t // 2][:, t % 2, :], ACT.Identity, bias=prior_t[:, t : t + 1]
                )
            h_bf.append(rows)

        h_codes = held("h_codes", [P, S], U32)
        h_s = held("h_s", [P, S], U8)

        def interleave(dst, rows):
            nc.vector.tensor_copy(
                dst.rearrange("p (c i t) -> p c t i", i=PACK, t=PACK),
                rows.rearrange("p t (c i) -> p c t i", i=PACK),
            )

        h_grouped = [held("h_grouped%d" % c, [P, CHUNK * PACK], BF16) for c in range(CHUNKS)]

        def quantize_h(c):
            cols = slice(c * CHUNK, (c + 1) * CHUNK)
            nc.vector.quantize_mx(out=h_codes[:, cols].bitcast(FP8X4), scales=h_s[:, cols], in_=h_grouped[c][:])

        v2_w = [held("v2_w%d" % g, [P, PACK, P], U32) for g in range(GROUPS)]

        def gather_questions(g):
            lc = K_PASS // LIST_COL
            nc.vector.tensor_copy(
                v2_w[g][:].rearrange("p t m -> p m t"), tab2_w[:].indirect(idx2[:, g * lc : (g + 1) * lc])
            )

        interleave(h_grouped[0][:], h_bf[0][:])
        interleave(h_grouped[1][:], h_bf[1][:])
        quantize_h(0)
        quantize_h(1)
        gather_questions(0)
        interleave(h_grouped[2][:], h_bf[2][:])
        interleave(h_grouped[3][:], h_bf[3][:])
        quantize_h(2)
        quantize_h(3)

        y_s = held("y_s", [P, GROUPS, S], U8)
        unit = 0
        for g in range(GROUPS):
            if g > 0:
                gather_questions(g)
            widths = [HALF, CHUNK, CHUNK] if g == GROUPS - 1 else [HALF, HALF]
            first = 0
            for width in widths:
                cols = slice(first, first + width)
                first += width
                y = rows32.tile([P, PACK, width], F32, name="y", tag="rows32")
                for t in range(PACK):
                    z = psum.tile([P, width], F32, name="bank%d" % (PACK * (unit % 2) + t))
                    nc.tensor.matmul_mx(
                        out=z[:],
                        lhsT=v2_w[g][:, t, :].bitcast(FP8X4), lhsT_scale=v2_s[:, g * K_PASS + t * P : g * K_PASS + (t + 1) * P],
                        rhs=h_codes[:, cols].bitcast(FP8X4), rhs_scale=h_s[:, cols],
                        start=True, stop=True,
                    )
                    prob = probs.tile([P, width], F32, name="prob")
                    nc.scalar.activation(prob[:], z[:], ACT.Tanh, bias=shift[:, g, t : t + 1], scale=0.5)
                    if t >= VECTOR_ROWS:
                        nc.scalar.activation(
                            y[:, t, :], prob[:], ACT.Identity,
                            bias=mid[:, g, t : t + 1], scale=gain[:, g, t : t + 1],
                        )
                    else:
                        nc.vector.tensor_scalar(
                            y[:, t, :], prob[:], gain[:, g, t : t + 1], mid[:, g, t : t + 1], ALU.mult, ALU.add
                        )
                rows = out_0[g * K_PASS : (g + 1) * K_PASS, cols].rearrange("(p t) j -> p t j", t=PACK)
                nc.sync.dma_start(rows, y[:])
                y_grouped = stage.tile([P, width * PACK], BF16, name="y_grouped", tag="grouped", align_bytes=64)
                interleave(y_grouped[:], y[:])
                y_codes = held("y_codes%d" % unit, [P, width], U32)
                nc.vector.quantize_mx(out=y_codes[:].bitcast(FP8X4), scales=y_s[:, g, cols], in_=y_grouped[:])
                nc.sync.dma_start(
                    out_1[g, :, cols, :].rearrange("p j t -> p (j t)").bitcast(I32), y_codes[:].bitcast(I32)
                )
                unit += 1
            if g > 0:
                done = slice(0, g + 1) if g < GROUPS - 1 else slice(g, g + 1)
                queue = nc.sync if g < GROUPS - 1 else nc.scalar
                for r in range(4):
                    queue.dma_start(
                        out_2[done, r:16:4, :].rearrange("g q j -> q g j").bitcast(I32),
                        y_s[r:P:QROWS, done, :].bitcast(I32),
                    )
